import numpy as np
import ml_dtypes


def mxq(x, axis, fmt="e4m3"):
    dtype, down = {"e4m3": (ml_dtypes.float8_e4m3fn, 7), "e5m2": (ml_dtypes.float8_e5m2, 14)}[fmt]
    v = np.moveaxis(np.asarray(x, np.float32).astype(ml_dtypes.bfloat16).astype(np.float64), axis, -1)
    blocks = v.reshape(v.shape[:-1] + (-1, 32))
    amax = np.abs(blocks).max(-1, keepdims=True)
    byte = np.maximum(np.where(amax > 0, np.frexp(amax)[1] - 1 + 127, 0) - down, 1)
    scale = np.exp2(byte - 127.0)
    codes = (blocks / scale).astype(np.float32).astype(dtype).astype(np.float64)
    return np.moveaxis((codes * scale).reshape(v.shape), -1, axis)


WIDE = False


def mx_kscale(k):
    if not WIDE:
        return np.ones(k)
    levels = np.array([18, -18])
    if k % 512:
        return np.exp2(np.random.permutation(np.resize(levels, k // 32))).repeat(32)
    a = np.empty((k // 512, 16))
    for p in range(k // 512):
        a[p, :8] = np.random.permutation(np.resize(levels, 8))
        for g in range(8):
            far = levels[np.abs(levels - a[p, g]) >= 10]
            a[p, g + 8] = far[np.random.randint(len(far))]
    return np.exp2(a.ravel()).repeat(32)


def f64(x):
    return np.asarray(x).astype(np.float64)


def striped(idx):
    return np.tile(np.asarray(idx).reshape(-1, 16).T, (8, 1)).astype(np.uint16)


def unstriped(offs):
    return offs[:16].T.reshape(-1).astype(np.int64)


B, N, T, D, DV = 2, 512, 2048, 1024, 512


def setup_inputs():
    n = np.random.standard_normal
    idx = np.random.permutation(T)[:B * N]
    v = mx_kscale(DV)[:, None]
    coarse = lambda x: x.astype(np.float32).astype(ml_dtypes.bfloat16).astype(np.float64)
    r = np.random.randint(8, 33, T) / 16.0
    return {
        "dyT": (coarse(n((DV, T))) * v).astype(np.float32),
        "hT": (np.random.randint(1, 32, (DV, T)) / 32.0).astype(np.float32),
        "ts": np.tile(r, (128, 1)).astype(np.float32),
        "wm": (n((B, DV, D)) / np.sqrt(DV) / v).astype(np.float32),
        "offs": striped(idx),
    }


def reference(dyT, hT, ts, wm, offs):
    idx = unstriped(offs)
    pick = lambda x: x[:, idx].reshape(x.shape[0], B, N).transpose(1, 0, 2)
    h = pick(f64(hT))
    dz = pick(f64(ts))[:, :1, :] * pick(f64(dyT)) * h * (1.0 - h)
    dx = mxq(f64(wm), 1, "e4m3").transpose(0, 2, 1) @ mxq(dz, 1, "e5m2")
    gx = np.zeros((D, T))
    gx[:, idx] = dx.transpose(1, 0, 2).reshape(D, B * N)
    return gx

@@ -1,0 +1,193 @@
+from contextlib import ExitStack
+
+import concourse.mybir as mybir
+from concourse.masks import make_identity
+
+B, N, T, D, DV = 2, 512, 2048, 1024, 512
+FLOPS = 2 * B * N * D * DV
+
+F32 = mybir.dt.float32
+BF16 = mybir.dt.bfloat16
+U32 = mybir.dt.uint32
+U16 = mybir.dt.uint16
+U8 = mybir.dt.uint8
+E4M3 = mybir.dt.float8_e4m3fn_x4
+E5M2 = mybir.dt.float8_e5m2_x4
+MULT = mybir.AluOpType.mult
+SUBTRACT = mybir.AluOpType.subtract
+COPY = mybir.ActivationFunctionType.Copy
+
+P = 128
+PACK = 4
+LIST_COLS = N // 16
+SLOT_BLOCKS = N // P
+D_BLOCKS = D // P
+W_LOAD = 512
+W_QUANT = 256
+WINDOWS = 3
+
+
+def tile_attend_gex_sig_x_kernel(tc, dyT, hT, ts, wm, offs, out):
+    nc = tc.nc
+    with ExitStack() as ctx:
+        keep = ctx.enter_context(tc.tile_pool(name="keep", bufs=1))
+        ring = ctx.enter_context(tc.tile_pool(name="ring", bufs=4))
+        psum = ctx.enter_context(tc.psum_pool(name="psum", bufs=2))
+
+        offsets = keep.tile([P, B * LIST_COLS], U16, name="offsets")
+        nc.sync.dma_start(offsets[:], offs)
+
+        def slots_of(b):
+            return offsets[:, b * LIST_COLS : (b + 1) * LIST_COLS]
+
+        ts_all = keep.tile([P, T], F32, name="ts_all")
+        ts_row = keep.tile([1, T], F32, name="ts_row")
+        nc.sync.dma_start(ts_row[:], ts[0:1, :])
+        nc.vector.memset(ts_all[:], 0.0)
+        nc.scalar.activation(ts_all[0:1, :], ts_row[:], COPY)
+
+        windows = [keep.tile([P, T], F32, name="window%d" % i) for i in range(WINDOWS)]
+        for window in windows:
+            nc.vector.memset(window[:], 0.0)
+
+        identity = keep.tile([P, P], F32, name="identity")
+        make_identity(nc, identity[:])
+
+        h_rows = hT.rearrange("(p t) c -> t p c", t=PACK)
+        dy_rows = dyT.rearrange("(p t) c -> t p c", t=PACK)
+        h_all = [keep.tile([P, T], F32, name="h_all%d" % t) for t in range(PACK)]
+        dy_all = [keep.tile([P, T], F32, name="dy_all%d" % t) for t in range(PACK)]
+        w_raw = {}
+
+        def load_w(b, c):
+            w_raw[b, c] = keep.tile([P, PACK, W_LOAD], F32, name="w_raw%d_%d" % (b, c))
+            cols = slice(c * W_LOAD, (c + 1) * W_LOAD)
+            nc.sync.dma_start(w_raw[b, c][:], wm[b].rearrange("(p t) d -> p t d", t=PACK)[:, :, cols])
+
+        for u in range(2):
+            for t in (2 * u, 2 * u + 1):
+                nc.sync.dma_start(h_all[t][:], h_rows[t])
+            for t in (2 * u, 2 * u + 1):
+                nc.sync.dma_start(dy_all[t][:], dy_rows[t])
+            load_w(u, 0)
+        load_w(0, 1)
+        load_w(1, 1)
+
+        ts_listed = keep.tile([P, B * N], F32, name="ts_listed")
+        nc.vector.tensor_copy(ts_listed[:], ts_all[:].indirect(offsets[:]))
+        neg_ts = keep.tile([P, B * SLOT_BLOCKS], F32, name="neg_ts")
+        for b in range(B):
+            turned_ts = psum.tile([P, SLOT_BLOCKS, P], F32, name="acc")
+            for s in range(SLOT_BLOCKS):
+                cols = slice(b * N + s * P, b * N + (s + 1) * P)
+                nc.tensor.transpose(turned_ts[:, s, :], ts_listed[:, cols], identity[:])
+            nc.scalar.activation(
+                neg_ts[:, b * SLOT_BLOCKS : (b + 1) * SLOT_BLOCKS], turned_ts[:, :, 0], COPY, scale=-1.0
+            )
+
+        dz_rows = [keep.tile([P, SLOT_BLOCKS, 2, P, 2], BF16, name="dz_rows%d" % b) for b in range(B)]
+        dz_codes = keep.tile([P, B, N], U32, name="dz_codes", align_bytes=64)
+        dz_scales = keep.tile([P, B, N], U8, name="dz_scales", align_bytes=64)
+        w_codes = keep.tile([P, B, D], U32, name="w_codes", align_bytes=64)
+        w_scales = keep.tile([P, B, D], U8, name="w_scales", align_bytes=64)
+
+        def form_dz(b, u):
+            slopes = []
+            for e in range(2):
+                h_listed = ring.tile([P, N], F32, name="h_listed")
+                nc.vector.tensor_copy(h_listed[:], h_all[2 * u + e][:].indirect(slots_of(b)))
+                slopes.append(h_listed)
+            for e in range(2):
+                neg_slope = ring.tile([P, N], F32, name="neg_slope")
+                nc.vector.scalar_tensor_tensor(neg_slope[:], slopes[e][:], 1.0, slopes[e][:], SUBTRACT, MULT)
+                slopes[e] = neg_slope
+            part = ring.tile([P, 2, N], F32, name="part")
+            for e in range(2):
+                nc.vector.tensor_tensor(part[:, e, :], dy_all[2 * u + e][:].indirect(slots_of(b)), slopes[e][:], MULT)
+            for half in range(2):
+                turned = psum.tile([P, 2, 2, P], F32, name="turned")
+                for i in range(2):
+                    s = 2 * half + i
+                    for e in range(2):
+                        nc.tensor.transpose(turned[:, i, e, :], part[:, e, s * P : (s + 1) * P], identity[:])
+                for i in range(2):
+                    s = 2 * half + i
+                    col = b * SLOT_BLOCKS + s
+                    nc.scalar.activation(
+                        dz_rows[b][:, s, u, :, :],
+                        turned[:, i, :, :].rearrange("s e p -> s p e"),
+                        COPY,
+                        scale=neg_ts[:, col : col + 1],
+                    )
+
+        def quantize_dz(b):
+            words = dz_rows[b][:].rearrange("s i u p e -> s (i u p e)").bitcast(F32)
+            grouped = keep.tile([P, N * PACK], BF16, name="dz_grouped%d" % b, align_bytes=64)
+            for half in range(2):
+                back = psum.tile([P, 2, 2 * P], F32, name="back")
+                for i in range(2):
+                    s = 2 * half + i
+                    for u in range(2):
+                        first = (2 * s + u) * P
+                        nc.tensor.transpose(back[:, u, i * P : (i + 1) * P], words[:, first : first + P], identity[:])
+                cols = slice(half * 2 * P * PACK, (half + 1) * 2 * P * PACK)
+                nc.scalar.copy(
+                    grouped[:, cols].bitcast(F32).rearrange("p (s u) -> p s u", u=2),
+                    back[:].rearrange("p u s -> p s u"),
+                )
+            nc.vector.quantize_mx(out=dz_codes[:, b, :].bitcast(E5M2), scales=dz_scales[:, b, :], in_=grouped[:])
+
+        def quantize_w(b, q):
+            grouped = ring.tile([P, W_QUANT, PACK], BF16, name="w_grouped", align_bytes=64)
+            c, first = divmod(q * W_QUANT, W_LOAD)
+            for i in range(W_QUANT // P):
+                cols = slice(first + i * P, first + (i + 1) * P)
+                nc.scalar.copy(grouped[:, i * P : (i + 1) * P, :], w_raw[b, c][:, :, cols].rearrange("p t d -> p d t"))
+            cols = slice(q * W_QUANT, (q + 1) * W_QUANT)
+            nc.vector.quantize_mx(
+                out=w_codes[:, b, cols].bitcast(E4M3),
+                scales=w_scales[:, b, cols],
+                in_=grouped[:].rearrange("p d t -> p (d t)"),
+            )
+
+        def product(b, j, staged):
+            acc = psum.tile([P, N], F32, name="acc")
+            cols = slice(j * P, (j + 1) * P)
+            nc.tensor.matmul_mx(
+                out=acc[:],
+                lhsT=w_codes[:, b, cols].bitcast(E4M3),
+                lhsT_scale=w_scales[:, b, cols],
+                rhs=dz_codes[:, b, :].bitcast(E5M2),
+                rhs_scale=dz_scales[:, b, :],
+                start=True,
+                stop=True,
+            )
+            nc.scalar.copy(staged[:, b * N : (b + 1) * N], acc[:])
+
+        def store(j):
+            nc.sync.dma_start(out[j * P : (j + 1) * P, :], windows[j % WINDOWS][:])
+
+        form_dz(0, 0)
+        quantize_w(0, 0)
+        form_dz(0, 1)
+        quantize_dz(0)
+        form_dz(1, 0)
+        quantize_w(1, 0)
+        form_dz(1, 1)
+        quantize_dz(1)
+
+        first_two = [ring.tile([P, B * N], F32, name="staged") for j in range(2)]
+        for b in range(B):
+            for j in range(2):
+                product(b, j, first_two[j])
+                nc.vector.tensor_copy(windows[j][:].indirect(slots_of(b)), first_two[j][:, b * N : (b + 1) * N])
+                if b == B - 1:
+                    store(j)
+        for j in range(2, D_BLOCKS):
+            staged = ring.tile([P, B * N], F32, name="staged")
+            for b in range(B):
+                if j % 2 == 0:
+                    quantize_w(b, j // 2)
+                product(b, j, staged)
+            nc.vector.tensor_copy(windows[j % WINDOWS][:].indirect(offsets[:]), staged[:])
+            store(j)

@@ -14,7 +14,6 @@ U8 = mybir.dt.uint8
 E4M3 = mybir.dt.float8_e4m3fn_x4
 E5M2 = mybir.dt.float8_e5m2_x4
 MULT = mybir.AluOpType.mult
-SUBTRACT = mybir.AluOpType.subtract
 COPY = mybir.ActivationFunctionType.Copy
 
 P = 128
@@ -22,8 +21,7 @@ PACK = 4
 LIST_COLS = N // 16
 SLOT_BLOCKS = N // P
 D_BLOCKS = D // P
-W_LOAD = 512
-W_QUANT = 256
+W_CHUNK = 2 * P
 WINDOWS = 3
 
 
@@ -32,84 +30,101 @@ def tile_attend_gex_sig_x_kernel(tc, dyT, hT, ts, wm, offs, out):
     with ExitStack() as ctx:
         keep = ctx.enter_context(tc.tile_pool(name="keep", bufs=1))
         ring = ctx.enter_context(tc.tile_pool(name="ring", bufs=4))
+        stage = ctx.enter_context(tc.tile_pool(name="stage", bufs=2))
         psum = ctx.enter_context(tc.psum_pool(name="psum", bufs=2))
+
+        def held(shape, dtype, name):
+            return keep.tile(shape, dtype, name=name, align_bytes=64)
 
         offsets = keep.tile([P, B * LIST_COLS], U16, name="offsets")
         nc.sync.dma_start(offsets[:], offs)
-
-        def slots_of(b):
-            return offsets[:, b * LIST_COLS : (b + 1) * LIST_COLS]
-
-        ts_all = keep.tile([P, T], F32, name="ts_all")
-        ts_row = keep.tile([1, T], F32, name="ts_row")
-        nc.sync.dma_start(ts_row[:], ts[0:1, :])
-        nc.vector.memset(ts_all[:], 0.0)
-        nc.scalar.activation(ts_all[0:1, :], ts_row[:], COPY)
-
-        windows = [keep.tile([P, T], F32, name="window%d" % i) for i in range(WINDOWS)]
-        for window in windows:
-            nc.vector.memset(window[:], 0.0)
-
-        identity = keep.tile([P, P], F32, name="identity")
+        ts_all = held([P, T], F32, "ts_all")
+        nc.sync.dma_start(ts_all[P - 1 : P, :], ts[P - 1 : P, :])
+        nc.vector.memset(ts_all[0 : P - 1, :], 0.0)
+        identity = held([P, P], F32, "identity")
         make_identity(nc, identity[:])
 
         h_rows = hT.rearrange("(p t) c -> t p c", t=PACK)
         dy_rows = dyT.rearrange("(p t) c -> t p c", t=PACK)
-        h_all = [keep.tile([P, T], F32, name="h_all%d" % t) for t in range(PACK)]
-        dy_all = [keep.tile([P, T], F32, name="dy_all%d" % t) for t in range(PACK)]
+        h_all = [held([P, T], F32, "h_all%d" % t) for t in range(PACK)]
+        dy_all = [held([P, T], F32, "dy_all%d" % t) for t in range(PACK)]
         w_raw = {}
 
-        def load_w(b, c):
-            w_raw[b, c] = keep.tile([P, PACK, W_LOAD], F32, name="w_raw%d_%d" % (b, c))
-            cols = slice(c * W_LOAD, (c + 1) * W_LOAD)
-            nc.sync.dma_start(w_raw[b, c][:], wm[b].rearrange("(p t) d -> p t d", t=PACK)[:, :, cols])
+        def load_w(b, q, slot):
+            w_raw[b, q] = held([P, PACK, W_CHUNK], F32, slot)
+            rows = wm[b].rearrange("(p t) d -> p t d", t=PACK)
+            nc.sync.dma_start(w_raw[b, q][:], rows[:, :, q * W_CHUNK : (q + 1) * W_CHUNK])
 
-        for u in range(2):
-            for t in (2 * u, 2 * u + 1):
-                nc.sync.dma_start(h_all[t][:], h_rows[t])
-            for t in (2 * u, 2 * u + 1):
-                nc.sync.dma_start(dy_all[t][:], dy_rows[t])
-            load_w(u, 0)
-        load_w(0, 1)
-        load_w(1, 1)
+        nc.sync.dma_start(h_all[0][:], h_rows[0])
+        nc.sync.dma_start(h_all[1][:], h_rows[1])
+        load_w(0, 0, "w_raw0")
+        nc.sync.dma_start(dy_all[0][:], dy_rows[0])
+        nc.sync.dma_start(dy_all[1][:], dy_rows[1])
+        nc.sync.dma_start(h_all[2][:], h_rows[2])
+        nc.sync.dma_start(h_all[3][:], h_rows[3])
+        nc.sync.dma_start(dy_all[2][:], dy_rows[2])
+        nc.sync.dma_start(dy_all[3][:], dy_rows[3])
+        load_w(0, 1, "w_raw1")
+        load_w(1, 0, "w_raw2")
+        load_w(1, 1, "w_raw3")
 
-        ts_listed = keep.tile([P, B * N], F32, name="ts_listed")
-        nc.vector.tensor_copy(ts_listed[:], ts_all[:].indirect(offsets[:]))
-        neg_ts = keep.tile([P, B * SLOT_BLOCKS], F32, name="neg_ts")
-        for b in range(B):
-            turned_ts = psum.tile([P, SLOT_BLOCKS, P], F32, name="acc")
-            for s in range(SLOT_BLOCKS):
-                cols = slice(b * N + s * P, b * N + (s + 1) * P)
-                nc.tensor.transpose(turned_ts[:, s, :], ts_listed[:, cols], identity[:])
-            nc.scalar.activation(
-                neg_ts[:, b * SLOT_BLOCKS : (b + 1) * SLOT_BLOCKS], turned_ts[:, :, 0], COPY, scale=-1.0
-            )
+        both = (0, 1)
 
-        dz_rows = [keep.tile([P, SLOT_BLOCKS, 2, P, 2], BF16, name="dz_rows%d" % b) for b in range(B)]
-        dz_codes = keep.tile([P, B, N], U32, name="dz_codes", align_bytes=64)
-        dz_scales = keep.tile([P, B, N], U8, name="dz_scales", align_bytes=64)
-        w_codes = keep.tile([P, B, D], U32, name="w_codes", align_bytes=64)
-        w_scales = keep.tile([P, B, D], U8, name="w_scales", align_bytes=64)
+        def span(experts):
+            return slice(experts[0] * N, (experts[-1] + 1) * N)
 
-        def form_dz(b, u):
-            slopes = []
-            for e in range(2):
-                h_listed = ring.tile([P, N], F32, name="h_listed")
-                nc.vector.tensor_copy(h_listed[:], h_all[2 * u + e][:].indirect(slots_of(b)))
-                slopes.append(h_listed)
-            for e in range(2):
-                neg_slope = ring.tile([P, N], F32, name="neg_slope")
-                nc.vector.scalar_tensor_tensor(neg_slope[:], slopes[e][:], 1.0, slopes[e][:], SUBTRACT, MULT)
-                slopes[e] = neg_slope
-            part = ring.tile([P, 2, N], F32, name="part")
-            for e in range(2):
-                nc.vector.tensor_tensor(part[:, e, :], dy_all[2 * u + e][:].indirect(slots_of(b)), slopes[e][:], MULT)
+        def listed(tile, experts):
+            return tile[:].indirect(offsets[:, experts[0] * LIST_COLS : (experts[-1] + 1) * LIST_COLS])
+
+        ts_cols = held([P, B * SLOT_BLOCKS], F32, "ts_cols")
+        h_listed = [held([P, B * N], F32, "h_listed%d" % t) for t in range(PACK)]
+        one_minus_h = [held([P, B * N], F32, "one_minus_h%d" % t) for t in range(PACK)]
+        dz_rows = [held([P, SLOT_BLOCKS, 2, P, 2], BF16, "dz_rows%d" % b) for b in range(B)]
+        dz_codes = held([P, B, N], U32, "dz_codes")
+        dz_scales = held([P, B, N], U8, "dz_scales")
+        slope = {}
+        part = {}
+        w_mx = {}
+        windows = []
+
+        def clear_window(slot):
+            window = held([P, T], F32, slot)
+            nc.gpsimd.memset(window[:], 0.0)
+            windows.append(window)
+
+        def gather_ts():
+            ts_listed = held([P, B * N], F32, "ts_listed")
+            nc.vector.tensor_copy(ts_listed[:], listed(ts_all, both))
+            for b in range(B):
+                turned_ts = psum.tile([P, SLOT_BLOCKS, P], F32, name="acc")
+                for s in range(SLOT_BLOCKS):
+                    cols = slice(b * N + s * P, b * N + (s + 1) * P)
+                    nc.tensor.transpose(turned_ts[:, s, :], ts_listed[:, cols], identity[:])
+                nc.scalar.copy(ts_cols[:, b * SLOT_BLOCKS : (b + 1) * SLOT_BLOCKS], turned_ts[:, :, P - 1])
+
+        def gather_h(t):
+            nc.vector.tensor_copy(h_listed[t][:], listed(h_all[t], both))
+            nc.scalar.activation(one_minus_h[t][:], h_listed[t][:], COPY, bias=1.0, scale=-1.0)
+
+        def form_slope(t, experts, dest):
+            cols = span(experts)
+            nc.vector.tensor_tensor(dest, h_listed[t][:, cols], one_minus_h[t][:, cols], MULT)
+            for i, b in enumerate(experts):
+                slope[t, b] = dest[:, i * N : (i + 1) * N]
+
+        def gather_dy(t, b, dest):
+            nc.vector.tensor_tensor(dest, listed(dy_all[t], (b,)), slope[t, b], MULT)
+            part[t, b] = dest
+
+        def round_dz(b, u, banks):
             for half in range(2):
-                turned = psum.tile([P, 2, 2, P], F32, name="turned")
-                for i in range(2):
-                    s = 2 * half + i
-                    for e in range(2):
-                        nc.tensor.transpose(turned[:, i, e, :], part[:, e, s * P : (s + 1) * P], identity[:])
+                turned = psum.tile([P, 2, 2, P], F32, name=banks)
+                for e in range(2):
+                    for i in range(2):
+                        s = 2 * half + i
+                        nc.tensor.transpose(
+                            turned[:, i, e, :], part[2 * u + e, b][:, s * P : (s + 1) * P], identity[:]
+                        )
                 for i in range(2):
                     s = 2 * half + i
                     col = b * SLOT_BLOCKS + s
@@ -117,77 +132,120 @@ def tile_attend_gex_sig_x_kernel(tc, dyT, hT, ts, wm, offs, out):
                         dz_rows[b][:, s, u, :, :],
                         turned[:, i, :, :].rearrange("s e p -> s p e"),
                         COPY,
-                        scale=neg_ts[:, col : col + 1],
+                        scale=ts_cols[:, col : col + 1],
                     )
 
-        def quantize_dz(b):
+        def turn_dz_back(b, halves):
             words = dz_rows[b][:].rearrange("s i u p e -> s (i u p e)").bitcast(F32)
-            grouped = keep.tile([P, N * PACK], BF16, name="dz_grouped%d" % b, align_bytes=64)
             for half in range(2):
                 back = psum.tile([P, 2, 2 * P], F32, name="back")
-                for i in range(2):
-                    s = 2 * half + i
-                    for u in range(2):
-                        first = (2 * s + u) * P
+                for u in range(2):
+                    for i in range(2):
+                        first = (2 * (2 * half + i) + u) * P
                         nc.tensor.transpose(back[:, u, i * P : (i + 1) * P], words[:, first : first + P], identity[:])
-                cols = slice(half * 2 * P * PACK, (half + 1) * 2 * P * PACK)
                 nc.scalar.copy(
-                    grouped[:, cols].bitcast(F32).rearrange("p (s u) -> p s u", u=2),
+                    halves[half].bitcast(F32).rearrange("p (s u) -> p s u", u=2),
                     back[:].rearrange("p u s -> p s u"),
                 )
-            nc.vector.quantize_mx(out=dz_codes[:, b, :].bitcast(E5M2), scales=dz_scales[:, b, :], in_=grouped[:])
 
-        def quantize_w(b, q):
-            grouped = ring.tile([P, W_QUANT, PACK], BF16, name="w_grouped", align_bytes=64)
-            c, first = divmod(q * W_QUANT, W_LOAD)
-            for i in range(W_QUANT // P):
-                cols = slice(first + i * P, first + (i + 1) * P)
-                nc.scalar.copy(grouped[:, i * P : (i + 1) * P, :], w_raw[b, c][:, :, cols].rearrange("p t d -> p d t"))
-            cols = slice(q * W_QUANT, (q + 1) * W_QUANT)
+        def quantize_dz(b, slots, grouped):
+            nc.vector.quantize_mx(out=dz_codes[:, b, slots].bitcast(E5M2), scales=dz_scales[:, b, slots], in_=grouped)
+
+        def quantize_w(b, q, slot):
+            grouped = ring.tile([P, W_CHUNK, PACK], BF16, name="w_grouped", align_bytes=64)
+            codes = held([P, W_CHUNK], U32, slot)
+            scales = held([P, W_CHUNK], U8, slot + "_scales")
+            for i in range(W_CHUNK // P):
+                cols = slice(i * P, (i + 1) * P)
+                nc.scalar.copy(grouped[:, cols, :], w_raw[b, q][:, :, cols].rearrange("p t d -> p d t"))
+                w_mx[b, 2 * q + i] = (codes[:, cols], scales[:, cols])
             nc.vector.quantize_mx(
-                out=w_codes[:, b, cols].bitcast(E4M3),
-                scales=w_scales[:, b, cols],
-                in_=grouped[:].rearrange("p d t -> p (d t)"),
+                out=codes[:].bitcast(E4M3), scales=scales[:], in_=grouped[:].rearrange("p d t -> p (d t)")
             )
 
         def product(b, j, staged):
             acc = psum.tile([P, N], F32, name="acc")
-            cols = slice(j * P, (j + 1) * P)
+            codes, scales = w_mx[b, j]
             nc.tensor.matmul_mx(
                 out=acc[:],
-                lhsT=w_codes[:, b, cols].bitcast(E4M3),
-                lhsT_scale=w_scales[:, b, cols],
+                lhsT=codes.bitcast(E4M3),
+                lhsT_scale=scales,
                 rhs=dz_codes[:, b, :].bitcast(E5M2),
                 rhs_scale=dz_scales[:, b, :],
                 start=True,
                 stop=True,
             )
-            nc.scalar.copy(staged[:, b * N : (b + 1) * N], acc[:])
+            nc.scalar.copy(staged, acc[:])
+
+        def scatter(j, experts, staged):
+            nc.vector.tensor_copy(listed(windows[j % WINDOWS], experts), staged)
 
         def store(j):
             nc.sync.dma_start(out[j * P : (j + 1) * P, :], windows[j % WINDOWS][:])
 
-        form_dz(0, 0)
-        quantize_w(0, 0)
-        form_dz(0, 1)
-        quantize_dz(0)
-        form_dz(1, 0)
-        quantize_w(1, 0)
-        form_dz(1, 1)
-        quantize_dz(1)
-
-        first_two = [ring.tile([P, B * N], F32, name="staged") for j in range(2)]
-        for b in range(B):
-            for j in range(2):
-                product(b, j, first_two[j])
-                nc.vector.tensor_copy(windows[j][:].indirect(slots_of(b)), first_two[j][:, b * N : (b + 1) * N])
-                if b == B - 1:
-                    store(j)
-        for j in range(2, D_BLOCKS):
-            staged = ring.tile([P, B * N], F32, name="staged")
+        half_width = N * PACK // 2
+        part_first = held([P, PACK, N], F32, "part_first")
+        gather_ts()
+        gather_h(0)
+        gather_h(1)
+        form_slope(0, both, held([P, B * N], F32, "h_all1")[:])
+        form_slope(1, both, held([P, B * N], F32, "slope1")[:])
+        clear_window("h_listed1")
+        gather_dy(0, 0, part_first[:, 0, :])
+        gather_dy(1, 0, part_first[:, 1, :])
+        round_dz(0, 0, "turned")
+        gather_h(2)
+        quantize_w(0, 0, "h_all2")
+        gather_h(3)
+        form_slope(2, both, held([P, B * N], F32, "h_all3")[:])
+        clear_window("h_listed2")
+        clear_window("one_minus_h2")
+        form_slope(3, (0,), held([P, N], F32, "late")[:])
+        gather_dy(2, 0, part_first[:, 2, :])
+        gather_dy(3, 0, part_first[:, 3, :])
+        round_dz(0, 1, "turned")
+        halves = [held([P, half_width], BF16, "dz_grouped0_%d" % half)[:] for half in range(2)]
+        turn_dz_back(0, halves)
+        late = held([P, 3, N], F32, "late")
+        gather_dy(0, 1, late[:, 0, :])
+        form_slope(3, (1,), late[:, 2, :])
+        gather_dy(1, 1, late[:, 1, :])
+        quantize_dz(0, slice(0, N // 2), halves[0])
+        quantize_dz(0, slice(N // 2, N), halves[1])
+        staged_first = [held([P, N], F32, "staged_first%d" % j) for j in range(2)]
+        product(0, 0, staged_first[0][:])
+        product(0, 1, staged_first[1][:])
+        round_dz(1, 0, "back")
+        latest = held([P, 2, N], F32, "dz_grouped0_1")
+        gather_dy(2, 1, latest[:, 0, :])
+        gather_dy(3, 1, latest[:, 1, :])
+        round_dz(1, 1, "turned")
+        grouped = held([P, N * PACK], BF16, "dz_grouped1")
+        turn_dz_back(1, [grouped[:, 0:half_width], grouped[:, half_width:]])
+        load_w(0, 2, "dy_all2")
+        load_w(1, 2, "dy_all3")
+        scatter(0, (0,), staged_first[0][:])
+        scatter(1, (0,), staged_first[1][:])
+        quantize_w(0, 1, "w_codes0")
+        quantize_dz(1, slice(0, N), grouped[:])
+        quantize_w(1, 0, "w_codes_first")
+        staged = held([P, N], F32, "dz_rows1")
+        product(0, 2, staged[:])
+        scatter(2, (0,), staged[:])
+        quantize_w(1, 1, "w_codes1")
+        load_w(0, 3, "w_raw1")
+        load_w(1, 3, "w_raw3")
+        for j in range(3):
+            staged = stage.tile([P, N], F32, name="staged")
+            product(1, j, staged[:])
+            scatter(j, (1,), staged[:])
+            store(j)
+        for j in range(3, D_BLOCKS):
+            staged = stage.tile([P, B * N], F32, name="staged")
             for b in range(B):
-                if j % 2 == 0:
-                    quantize_w(b, j // 2)
-                product(b, j, staged)
-            nc.vector.tensor_copy(windows[j % WINDOWS][:].indirect(offsets[:]), staged[:])
+                product(b, j, staged[:, b * N : (b + 1) * N])
+            if j % 2 == 1 and j + 1 < D_BLOCKS:
+                for b in range(B):
+                    quantize_w(b, (j + 1) // 2, "w_codes%d" % b)
+            scatter(j, both, staged[:])
             store(j)

@@ -55,15 +55,11 @@ def tile_attend_gex_sig_x_kernel(tc, dyT, hT, ts, wm, offs, out):
             rows = wm[b].rearrange("(p t) d -> p t d", t=PACK)
             nc.sync.dma_start(w_raw[b, q][:], rows[:, :, q * W_CHUNK : (q + 1) * W_CHUNK])
 
-        nc.sync.dma_start(h_all[0][:], h_rows[0])
-        nc.sync.dma_start(h_all[1][:], h_rows[1])
+        for t in range(PACK):
+            nc.sync.dma_start(h_all[t][:], h_rows[t])
+        for t in range(PACK):
+            nc.sync.dma_start(dy_all[t][:], dy_rows[t])
         load_w(0, 0, "w_raw0")
-        nc.sync.dma_start(dy_all[0][:], dy_rows[0])
-        nc.sync.dma_start(dy_all[1][:], dy_rows[1])
-        nc.sync.dma_start(h_all[2][:], h_rows[2])
-        nc.sync.dma_start(h_all[3][:], h_rows[3])
-        nc.sync.dma_start(dy_all[2][:], dy_rows[2])
-        nc.sync.dma_start(dy_all[3][:], dy_rows[3])
         load_w(0, 1, "w_raw1")
         load_w(1, 0, "w_raw2")
         load_w(1, 1, "w_raw3")
@@ -87,9 +83,9 @@ def tile_attend_gex_sig_x_kernel(tc, dyT, hT, ts, wm, offs, out):
         w_mx = {}
         windows = []
 
-        def clear_window(slot):
+        def clear_window(engine, slot):
             window = held([P, T], F32, slot)
-            nc.gpsimd.memset(window[:], 0.0)
+            engine.memset(window[:], 0.0)
             windows.append(window)
 
         def gather_ts():
@@ -102,15 +98,15 @@ def tile_attend_gex_sig_x_kernel(tc, dyT, hT, ts, wm, offs, out):
                     nc.tensor.transpose(turned_ts[:, s, :], ts_listed[:, cols], identity[:])
                 nc.scalar.copy(ts_cols[:, b * SLOT_BLOCKS : (b + 1) * SLOT_BLOCKS], turned_ts[:, :, P - 1])
 
-        def gather_h(t):
-            nc.vector.tensor_copy(h_listed[t][:], listed(h_all[t], both))
-            nc.scalar.activation(one_minus_h[t][:], h_listed[t][:], COPY, bias=1.0, scale=-1.0)
+        def gather_h(t, b):
+            cols = span((b,))
+            nc.vector.tensor_copy(h_listed[t][:, cols], listed(h_all[t], (b,)))
+            nc.scalar.activation(one_minus_h[t][:, cols], h_listed[t][:, cols], COPY, bias=1.0, scale=-1.0)
 
-        def form_slope(t, experts, dest):
-            cols = span(experts)
-            nc.vector.tensor_tensor(dest, h_listed[t][:, cols], one_minus_h[t][:, cols], MULT)
-            for i, b in enumerate(experts):
-                slope[t, b] = dest[:, i * N : (i + 1) * N]
+        def form_slope(engine, t, b, dest):
+            cols = span((b,))
+            engine.tensor_tensor(dest, h_listed[t][:, cols], one_minus_h[t][:, cols], MULT)
+            slope[t, b] = dest
 
         def gather_dy(t, b, dest):
             nc.vector.tensor_tensor(dest, listed(dy_all[t], (b,)), slope[t, b], MULT)
@@ -151,13 +147,16 @@ def tile_attend_gex_sig_x_kernel(tc, dyT, hT, ts, wm, offs, out):
         def quantize_dz(b, slots, grouped):
             nc.vector.quantize_mx(out=dz_codes[:, b, slots].bitcast(E5M2), scales=dz_scales[:, b, slots], in_=grouped)
 
-        def quantize_w(b, q, slot):
+        def quantize_w(b, q, slot, on_vector=False):
             grouped = ring.tile([P, W_CHUNK, PACK], BF16, name="w_grouped", align_bytes=64)
+            if on_vector:
+                nc.vector.tensor_copy(grouped[:], w_raw[b, q][:].rearrange("p t d -> p d t"))
             codes = held([P, W_CHUNK], U32, slot)
             scales = held([P, W_CHUNK], U8, slot + "_scales")
             for i in range(W_CHUNK // P):
                 cols = slice(i * P, (i + 1) * P)
-                nc.scalar.copy(grouped[:, cols, :], w_raw[b, q][:, :, cols].rearrange("p t d -> p d t"))
+                if not on_vector:
+                    nc.scalar.copy(grouped[:, cols, :], w_raw[b, q][:, :, cols].rearrange("p t d -> p d t"))
                 w_mx[b, 2 * q + i] = (codes[:, cols], scales[:, cols])
             nc.vector.quantize_mx(
                 out=codes[:].bitcast(E4M3), scales=scales[:], in_=grouped[:].rearrange("p d t -> p (d t)")
@@ -185,31 +184,29 @@ def tile_attend_gex_sig_x_kernel(tc, dyT, hT, ts, wm, offs, out):
 
         half_width = N * PACK // 2
         part_first = held([P, PACK, N], F32, "part_first")
+        clear_window(nc.vector, "window0")
         gather_ts()
-        gather_h(0)
-        gather_h(1)
-        form_slope(0, both, held([P, B * N], F32, "h_all1")[:])
-        form_slope(1, both, held([P, B * N], F32, "slope1")[:])
-        clear_window("h_listed1")
+        for t in range(PACK):
+            for b in range(B):
+                gather_h(t, b)
+                if t < PACK - 1:
+                    form_slope(nc.gpsimd, t, b, held([P, N], F32, "slope%d_%d" % (t, b))[:])
+        form_slope(nc.vector, 3, 0, held([P, N], F32, "late")[:])
         gather_dy(0, 0, part_first[:, 0, :])
+        clear_window(nc.gpsimd, "slope0_0")
+        gather_dy(0, 1, held([P, N], F32, "part0_1")[:])
+        clear_window(nc.gpsimd, "slope0_1")
         gather_dy(1, 0, part_first[:, 1, :])
         round_dz(0, 0, "turned")
-        gather_h(2)
-        quantize_w(0, 0, "h_all2")
-        gather_h(3)
-        form_slope(2, both, held([P, B * N], F32, "h_all3")[:])
-        clear_window("h_listed2")
-        clear_window("one_minus_h2")
-        form_slope(3, (0,), held([P, N], F32, "late")[:])
         gather_dy(2, 0, part_first[:, 2, :])
         gather_dy(3, 0, part_first[:, 3, :])
         round_dz(0, 1, "turned")
         halves = [held([P, half_width], BF16, "dz_grouped0_%d" % half)[:] for half in range(2)]
         turn_dz_back(0, halves)
-        late = held([P, 3, N], F32, "late")
-        gather_dy(0, 1, late[:, 0, :])
-        form_slope(3, (1,), late[:, 2, :])
-        gather_dy(1, 1, late[:, 1, :])
+        late = held([P, 2, N], F32, "late")
+        gather_dy(1, 1, late[:, 0, :])
+        form_slope(nc.vector, 3, 1, late[:, 1, :])
+        quantize_w(0, 0, "w_codes_a", on_vector=True)
         quantize_dz(0, slice(0, N // 2), halves[0])
         quantize_dz(0, slice(N // 2, N), halves[1])
         staged_first = [held([P, N], F32, "staged_first%d" % j) for j in range(2)]

@@ -184,13 +184,13 @@ def tile_attend_gex_sig_x_kernel(tc, dyT, hT, ts, wm, offs, out):
 
         half_width = N * PACK // 2
         part_first = held([P, PACK, N], F32, "part_first")
-        clear_window(nc.vector, "window0")
         gather_ts()
         for t in range(PACK):
             for b in range(B):
                 gather_h(t, b)
                 if t < PACK - 1:
                     form_slope(nc.gpsimd, t, b, held([P, N], F32, "slope%d_%d" % (t, b))[:])
+        clear_window(nc.gpsimd, "one_minus_h2")
         form_slope(nc.vector, 3, 0, held([P, N], F32, "late")[:])
         gather_dy(0, 0, part_first[:, 0, :])
         clear_window(nc.gpsimd, "slope0_0")

from contextlib import ExitStack

import concourse.mybir as mybir
from concourse.masks import make_identity

B, N, T, D, DV = 2, 512, 2048, 1024, 512
FLOPS = 2 * B * N * D * DV

F32 = mybir.dt.float32
BF16 = mybir.dt.bfloat16
U32 = mybir.dt.uint32
U16 = mybir.dt.uint16
U8 = mybir.dt.uint8
E4M3 = mybir.dt.float8_e4m3fn_x4
E5M2 = mybir.dt.float8_e5m2_x4
MULT = mybir.AluOpType.mult
COPY = mybir.ActivationFunctionType.Copy

P = 128
PACK = 4
LIST_COLS = N // 16
SLOT_BLOCKS = N // P
D_BLOCKS = D // P
W_CHUNK = 2 * P
WINDOWS = 3


def tile_attend_gex_sig_x_kernel(tc, dyT, hT, ts, wm, offs, out):
    nc = tc.nc
    with ExitStack() as ctx:
        keep = ctx.enter_context(tc.tile_pool(name="keep", bufs=1))
        ring = ctx.enter_context(tc.tile_pool(name="ring", bufs=4))
        stage = ctx.enter_context(tc.tile_pool(name="stage", bufs=2))
        psum = ctx.enter_context(tc.psum_pool(name="psum", bufs=2))

        def held(shape, dtype, name):
            return keep.tile(shape, dtype, name=name, align_bytes=64)

        offsets = keep.tile([P, B * LIST_COLS], U16, name="offsets")
        nc.sync.dma_start(offsets[:], offs)
        ts_all = held([P, T], F32, "ts_all")
        nc.sync.dma_start(ts_all[P - 1 : P, :], ts[P - 1 : P, :])
        nc.vector.memset(ts_all[0 : P - 1, :], 0.0)
        identity = held([P, P], F32, "identity")
        make_identity(nc, identity[:])

        h_rows = hT.rearrange("(p t) c -> t p c", t=PACK)
        dy_rows = dyT.rearrange("(p t) c -> t p c", t=PACK)
        h_all = [held([P, T], F32, "h_all%d" % t) for t in range(PACK)]
        dy_all = [held([P, T], F32, "dy_all%d" % t) for t in range(PACK)]
        w_raw = {}

        def load_w(b, q, slot):
            w_raw[b, q] = held([P, PACK, W_CHUNK], F32, slot)
            rows = wm[b].rearrange("(p t) d -> p t d", t=PACK)
            nc.sync.dma_start(w_raw[b, q][:], rows[:, :, q * W_CHUNK : (q + 1) * W_CHUNK])

        for t in range(PACK):
            nc.sync.dma_start(h_all[t][:], h_rows[t])
        for t in range(PACK):
            nc.sync.dma_start(dy_all[t][:], dy_rows[t])
        load_w(0, 0, "w_raw0")
        load_w(0, 1, "w_raw1")
        load_w(1, 0, "w_raw2")
        load_w(1, 1, "w_raw3")

        both = (0, 1)

        def span(experts):
            return slice(experts[0] * N, (experts[-1] + 1) * N)

        def listed(tile, experts):
            return tile[:].indirect(offsets[:, experts[0] * LIST_COLS : (experts[-1] + 1) * LIST_COLS])

        ts_cols = held([P, B * SLOT_BLOCKS], F32, "ts_cols")
        h_listed = [held([P, B * N], F32, "h_listed%d" % t) for t in range(PACK)]
        one_minus_h = [held([P, B * N], F32, "one_minus_h%d" % t) for t in range(PACK)]
        dz_rows = [held([P, SLOT_BLOCKS, 2, P, 2], BF16, "dz_rows%d" % b) for b in range(B)]
        dz_codes = held([P, B, N], U32, "dz_codes")
        dz_scales = held([P, B, N], U8, "dz_scales")
        slope = {}
        part = {}
        w_mx = {}
        windows = []

        def clear_window(engine, slot):
            window = held([P, T], F32, slot)
            engine.memset(window[:], 0.0)
            windows.append(window)

        def gather_ts():
            ts_listed = held([P, B * N], F32, "ts_listed")
            nc.vector.tensor_copy(ts_listed[:], listed(ts_all, both))
            for b in range(B):
                turned_ts = psum.tile([P, SLOT_BLOCKS, P], F32, name="acc")
                for s in range(SLOT_BLOCKS):
                    cols = slice(b * N + s * P, b * N + (s + 1) * P)
                    nc.tensor.transpose(turned_ts[:, s, :], ts_listed[:, cols], identity[:])
                nc.scalar.copy(ts_cols[:, b * SLOT_BLOCKS : (b + 1) * SLOT_BLOCKS], turned_ts[:, :, P - 1])

        def gather_h(t, b):
            cols = span((b,))
            nc.vector.tensor_copy(h_listed[t][:, cols], listed(h_all[t], (b,)))
            nc.scalar.activation(one_minus_h[t][:, cols], h_listed[t][:, cols], COPY, bias=1.0, scale=-1.0)

        def form_slope(engine, t, b, dest):
            cols = span((b,))
            engine.tensor_tensor(dest, h_listed[t][:, cols], one_minus_h[t][:, cols], MULT)
            slope[t, b] = dest

        def gather_dy(t, b, dest):
            nc.vector.tensor_tensor(dest, listed(dy_all[t], (b,)), slope[t, b], MULT)
            part[t, b] = dest

        def round_dz(b, u, banks):
            for half in range(2):
                turned = psum.tile([P, 2, 2, P], F32, name=banks)
                for e in range(2):
                    for i in range(2):
                        s = 2 * half + i
                        nc.tensor.transpose(
                            turned[:, i, e, :], part[2 * u + e, b][:, s * P : (s + 1) * P], identity[:]
                        )
                for i in range(2):
                    s = 2 * half + i
                    col = b * SLOT_BLOCKS + s
                    nc.scalar.activation(
                        dz_rows[b][:, s, u, :, :],
                        turned[:, i, :, :].rearrange("s e p -> s p e"),
                        COPY,
                        scale=ts_cols[:, col : col + 1],
                    )

        def turn_dz_back(b, halves):
            words = dz_rows[b][:].rearrange("s i u p e -> s (i u p e)").bitcast(F32)
            for half in range(2):
                back = psum.tile([P, 2, 2 * P], F32, name="back")
                for u in range(2):
                    for i in range(2):
                        first = (2 * (2 * half + i) + u) * P
                        nc.tensor.transpose(back[:, u, i * P : (i + 1) * P], words[:, first : first + P], identity[:])
                nc.scalar.copy(
                    halves[half].bitcast(F32).rearrange("p (s u) -> p s u", u=2),
                    back[:].rearrange("p u s -> p s u"),
                )

        def quantize_dz(b, slots, grouped):
            nc.vector.quantize_mx(out=dz_codes[:, b, slots].bitcast(E5M2), scales=dz_scales[:, b, slots], in_=grouped)

        def quantize_w(b, q, slot, on_vector=False):
            grouped = ring.tile([P, W_CHUNK, PACK], BF16, name="w_grouped", align_bytes=64)
            if on_vector:
                nc.vector.tensor_copy(grouped[:], w_raw[b, q][:].rearrange("p t d -> p d t"))
            codes = held([P, W_CHUNK], U32, slot)
            scales = held([P, W_CHUNK], U8, slot + "_scales")
            for i in range(W_CHUNK // P):
                cols = slice(i * P, (i + 1) * P)
                if not on_vector:
                    nc.scalar.copy(grouped[:, cols, :], w_raw[b, q][:, :, cols].rearrange("p t d -> p d t"))
                w_mx[b, 2 * q + i] = (codes[:, cols], scales[:, cols])
            nc.vector.quantize_mx(
                out=codes[:].bitcast(E4M3), scales=scales[:], in_=grouped[:].rearrange("p d t -> p (d t)")
            )

        def product(b, j, staged):
            acc = psum.tile([P, N], F32, name="acc")
            codes, scales = w_mx[b, j]
            nc.tensor.matmul_mx(
                out=acc[:],
                lhsT=codes.bitcast(E4M3),
                lhsT_scale=scales,
                rhs=dz_codes[:, b, :].bitcast(E5M2),
                rhs_scale=dz_scales[:, b, :],
                start=True,
                stop=True,
            )
            nc.scalar.copy(staged, acc[:])

        def scatter(j, experts, staged):
            nc.vector.tensor_copy(listed(windows[j % WINDOWS], experts), staged)

        def store(j):
            nc.sync.dma_start(out[j * P : (j + 1) * P, :], windows[j % WINDOWS][:])

        half_width = N * PACK // 2
        part_first = held([P, PACK, N], F32, "part_first")
        gather_ts()
        for t in range(PACK):
            for b in range(B):
                gather_h(t, b)
                if t < PACK - 1:
                    form_slope(nc.gpsimd, t, b, held([P, N], F32, "slope%d_%d" % (t, b))[:])
        clear_window(nc.gpsimd, "one_minus_h2")
        form_slope(nc.vector, 3, 0, held([P, N], F32, "late")[:])
        gather_dy(0, 0, part_first[:, 0, :])
        clear_window(nc.gpsimd, "slope0_0")
        gather_dy(0, 1, held([P, N], F32, "part0_1")[:])
        clear_window(nc.gpsimd, "slope0_1")
        gather_dy(1, 0, part_first[:, 1, :])
        round_dz(0, 0, "turned")
        gather_dy(2, 0, part_first[:, 2, :])
        gather_dy(3, 0, part_first[:, 3, :])
        round_dz(0, 1, "turned")
        halves = [held([P, half_width], BF16, "dz_grouped0_%d" % half)[:] for half in range(2)]
        turn_dz_back(0, halves)
        late = held([P, 2, N], F32, "late")
        gather_dy(1, 1, late[:, 0, :])
        form_slope(nc.vector, 3, 1, late[:, 1, :])
        quantize_w(0, 0, "w_codes_a", on_vector=True)
        quantize_dz(0, slice(0, N // 2), halves[0])
        quantize_dz(0, slice(N // 2, N), halves[1])
        staged_first = [held([P, N], F32, "staged_first%d" % j) for j in range(2)]
        product(0, 0, staged_first[0][:])
        product(0, 1, staged_first[1][:])
        round_dz(1, 0, "back")
        latest = held([P, 2, N], F32, "dz_grouped0_1")
        gather_dy(2, 1, latest[:, 0, :])
        gather_dy(3, 1, latest[:, 1, :])
        round_dz(1, 1, "turned")
        grouped = held([P, N * PACK], BF16, "dz_grouped1")
        turn_dz_back(1, [grouped[:, 0:half_width], grouped[:, half_width:]])
        load_w(0, 2, "dy_all2")
        load_w(1, 2, "dy_all3")
        scatter(0, (0,), staged_first[0][:])
        scatter(1, (0,), staged_first[1][:])
        quantize_w(0, 1, "w_codes0")
        quantize_dz(1, slice(0, N), grouped[:])
        quantize_w(1, 0, "w_codes_first")
        staged = held([P, N], F32, "dz_rows1")
        product(0, 2, staged[:])
        scatter(2, (0,), staged[:])
        quantize_w(1, 1, "w_codes1")
        load_w(0, 3, "w_raw1")
        load_w(1, 3, "w_raw3")
        for j in range(3):
            staged = stage.tile([P, N], F32, name="staged")
            product(1, j, staged[:])
            scatter(j, (1,), staged[:])
            store(j)
        for j in range(3, D_BLOCKS):
            staged = stage.tile([P, B * N], F32, name="staged")
            for b in range(B):
                product(b, j, staged[:, b * N : (b + 1) * N])
            if j % 2 == 1 and j + 1 < D_BLOCKS:
                for b in range(B):
                    quantize_w(b, (j + 1) // 2, "w_codes%d" % b)
            scatter(j, both, staged[:])
            store(j)
